import numpy as np
import ml_dtypes


def mxq(x, axis, fmt="e4m3"):
    dtype, down = {"e4m3": (ml_dtypes.float8_e4m3fn, 7), "e5m2": (ml_dtypes.float8_e5m2, 14)}[fmt]
    v = np.moveaxis(np.asarray(x, np.float32).astype(ml_dtypes.bfloat16).astype(np.float64), axis, -1)
    blocks = v.reshape(v.shape[:-1] + (-1, 32))
    amax = np.abs(blocks).max(-1, keepdims=True)
    byte = np.maximum(np.where(amax > 0, np.frexp(amax)[1] - 1 + 127, 0) - down, 1)
    scale = np.exp2(byte - 127.0)
    codes = (blocks / scale).astype(np.float32).astype(dtype).astype(np.float64)
    return np.moveaxis((codes * scale).reshape(v.shape), -1, axis)


WIDE = False


def mx_kscale(k):
    if not WIDE:
        return np.ones(k)
    levels = np.array([10, -10, 5, -5, 0])
    if k % 512:
        return np.exp2(np.random.permutation(np.resize(levels, k // 32))).repeat(32)
    a = np.empty((k // 512, 16))
    for p in range(k // 512):
        a[p, :8] = np.random.permutation(np.resize(levels, 8))
        for g in range(8):
            far = levels[np.abs(levels - a[p, g]) >= 10]
            a[p, g + 8] = far[np.random.randint(len(far))]
    return np.exp2(a.ravel()).repeat(32)


BF16 = ml_dtypes.bfloat16


def bf(x):
    return np.asarray(x, np.float32).astype(BF16)


def f64(x):
    return np.asarray(x).astype(np.float64)


E2M1 = np.array([0.0, 0.5, 1.0, 1.5, 2.0, 3.0, 4.0, 6.0, -0.0, -0.5, -1.0, -1.5, -2.0, -3.0, -4.0, -6.0])


def pack_weight(w, fmt):
    k, n = w.shape
    w = f64(bf(w)).reshape(k // 32, 32, n)
    amax = np.abs(w).max(1)
    if fmt == "e4m3":
        byte = np.frexp(amax)[1] - 1 + 127 - 7
    else:
        mant, ex = np.frexp(amax / 6.0)
        byte = np.where(mant > 0.5, ex, ex - 1) + 127
    byte = np.clip(np.where(amax > 0, byte, 1), 1, 254)
    scaled = (w * np.exp2(127.0 - byte)[:, None, :]).reshape(k, n).astype(np.float32)
    by_word = np.ascontiguousarray(scaled.reshape(k // 512, 128, 4, n).transpose(0, 1, 3, 2))
    if fmt == "e4m3":
        words = by_word.astype(ml_dtypes.float8_e4m3fn).view(np.uint8)
    else:
        c = by_word.astype(ml_dtypes.float4_e2m1fn).view(np.uint8) & 0xF
        words = c[..., 0::2] | (c[..., 1::2] << 4)
    return np.ascontiguousarray(words), np.ascontiguousarray(byte.astype(np.uint8).reshape(k // 512, 16, n))


def unpack_weight(words, scales, fmt):
    g, p, n, _ = words.shape
    if fmt == "e4m3":
        vals = np.ascontiguousarray(words).view(ml_dtypes.float8_e4m3fn).astype(np.float64)
    else:
        nib = np.empty((g, p, n, 4), np.uint8)
        nib[..., 0::2] = words & 0xF
        nib[..., 1::2] = words >> 4
        vals = E2M1[nib]
    vals = vals * np.repeat(np.exp2(scales.astype(np.float64) - 127.0), 8, axis=1)[..., None]
    return vals.transpose(0, 1, 3, 2).reshape(g * 512, n)


T, D, F, R, E = 2048, 1024, 1024, 128, 8
ER = E * R


def draw0():
    u = mx_kscale(D)
    t = mx_kscale(ER)
    x = bf(np.random.standard_normal((T, D)) * u)
    w0_words, w0_scales = pack_weight(np.random.standard_normal((D, F)) / np.sqrt(D) / u[:, None], "e4m3")
    wa_words, wa_scales = pack_weight(np.random.standard_normal((D, R)) / np.sqrt(D) / u[:, None], "e4m3")
    c = bf(np.random.standard_normal((E, R)))
    s = bf((1.0 + 0.1 * np.random.standard_normal(ER)) * t)
    wb_words, wb_scales = pack_weight(np.random.standard_normal((ER, F)) / np.sqrt(R) / t[:, None], "e4m3")
    return {"x": x,
            "w0_words": w0_words, "w0_scales": w0_scales,
            "wa_words": wa_words, "wa_scales": wa_scales,
            "c": c,
            "s": s,
            "wb_words": wb_words, "wb_scales": wb_scales}


def prototype_gate(a, c):
    diff = a[:, None, :] - c[None, :, :]
    logits = -np.sum(diff * diff, axis=-1) / 16.0
    e = np.exp(logits - logits.max(-1, keepdims=True))
    return e / e.sum(-1, keepdims=True)


def core(x, w0_words, w0_scales, wa_words, wa_scales, c, s, wb_words, wb_scales):
    xq = mxq(f64(x), 1, "e4m3")
    a = xq @ unpack_weight(wa_words, wa_scales, "e4m3")
    g = prototype_gate(a, f64(c))
    wb = unpack_weight(wb_words, wb_scales, "e4m3")
    z = (g[:, :, None] * a[:, None, :]).reshape(x.shape[0], wb.shape[0])
    zs = z * f64(s)[None, :]
    low = mxq(zs, 1, "e4m3") @ wb
    return (xq @ unpack_weight(w0_words, w0_scales, "e4m3")) + 1.5 * low


def e4m3fn_bytes(y):
    return np.clip(np.asarray(y, np.float64), -448.0, 448.0).astype(np.float32).astype(ml_dtypes.float8_e4m3fn).view(np.uint8)


def e4m3fn_values(b):
    return np.asarray(b, np.uint8).view(ml_dtypes.float8_e4m3fn).astype(np.float64)


def setup_inputs():
    d = draw0()
    x0 = np.asarray(d['x']).astype(np.float64)
    s = (np.max(np.abs(x0), axis=(0,), keepdims=True) / 448.0).astype(np.float32)
    out = {}
    for k, v in d.items():
        if k == 'x':
            out['x_bytes'] = e4m3fn_bytes(x0 / s.astype(np.float64))
            out['x_scale'] = s
        else:
            out[k] = v
    return out


def reference(x_bytes, x_scale, w0_words, w0_scales, wa_words, wa_scales, c, s, wb_words, wb_scales):
    return core(e4m3fn_values(x_bytes) * x_scale.astype(np.float64), w0_words, w0_scales, wa_words, wa_scales, c, s, wb_words, wb_scales)

@@ -1,0 +1,360 @@
+from contextlib import ExitStack
+
+import concourse.mybir as mybir
+from concourse.masks import make_identity
+
+T, D, F, R, E = 2048, 1024, 1024, 128, 8
+FLOPS = 2 * T * (D * F + D * R + E * R * F)
+
+F32 = mybir.dt.float32
+BF16 = mybir.dt.bfloat16
+U32 = mybir.dt.uint32
+I32 = mybir.dt.int32
+U8 = mybir.dt.uint8
+FP8 = mybir.dt.float8_e4m3fn
+FP8X4 = mybir.dt.float8_e4m3fn_x4
+ALU = mybir.AluOpType
+ACT = mybir.ActivationFunctionType
+AX = mybir.AxisListType
+
+P = 128
+J = 2
+NT = P * J
+CHUNKS = T // NT
+G = 2
+PACK = 4
+HALF = 512
+SP = 4
+OB = 2
+ZV = 4
+
+
+def tile_hydraloraprototyperouted_w8_kernel(
+    tc, x_bytes, x_scale, w0_words, w0_scales, wa_words, wa_scales, c, s, wb_words, wb_scales, out
+):
+    nc = tc.nc
+    with ExitStack() as ctx:
+        const = ctx.enter_context(tc.tile_pool(name="const", bufs=1))
+        work = ctx.enter_context(tc.tile_pool(name="work", bufs=2))
+        psum = ctx.enter_context(tc.psum_pool(name="psum", bufs=1))
+
+        x_in = []
+        xs = const.tile([P, D], F32, name="xs", align_bytes=64)
+        w0sc = const.tile([P, F], U8, name="w0sc", align_bytes=64)
+        wbsc = const.tile([P, F], U8, name="wbsc", align_bytes=64)
+        wasc = const.tile([P, R], U8, name="wasc", align_bytes=64)
+        cf = const.tile([P, P], F32, name="cf")
+        for t in (wasc, w0sc, wbsc):
+            nc.gpsimd.memset(t[:].bitcast(I32), 0)
+        nc.gpsimd.memset(cf[:], 0.0)
+        ident = const.tile([P, P], F32, name="ident")
+        make_identity(nc, ident[:])
+        fours = const.tile([P, P], F32, name="fours")
+        nc.gpsimd.memset(fours[:], 4.0)
+
+        def load_x(i):
+            t = const.tile([P, J, D], U8, name="x_in%d" % i, align_bytes=64)
+            nc.sync.dma_start(out=t[:], in_=x_bytes[NT * i : NT * (i + 1), :].rearrange("(p j) k -> p j k", j=J))
+            x_in.append(t)
+
+        def load_scales(tile, dram):
+            for q in range(4):
+                nc.sync.dma_start(
+                    out=tile[32 * q : 32 * q + 8, :].bitcast(I32),
+                    in_=dram[:, 4 * q : 4 * q + 4, :].bitcast(I32),
+                )
+
+        load_x(0)
+        nc.sync.dma_start(out=xs[:], in_=x_scale.rearrange("o k -> (o k)").partition_broadcast(P))
+        load_scales(wasc, wa_scales)
+        wa = const.tile([P, G, R * PACK], U8, name="wa", align_bytes=64)
+        nc.sync.dma_start(out=wa[:], in_=wa_words.rearrange("g p n t -> p g (n t)"))
+        load_scales(w0sc, w0_scales)
+        load_scales(wbsc, wb_scales)
+        c_in = const.tile([E, R], BF16, name="c_in")
+        nc.sync.dma_start(out=c_in[:], in_=c)
+        s_in = const.tile([P, G, PACK], BF16, name="s_in")
+        nc.sync.dma_start(out=s_in[:], in_=s.rearrange("(g p t) -> p g t", p=P, t=PACK))
+        load_x(1)
+        w0 = []
+        wb = []
+
+        def load_w(name, dram, h):
+            t = const.tile([P, G, HALF * PACK], U8, name="%s%d" % (name, h), align_bytes=64)
+            nc.sync.dma_start(
+                out=t[:], in_=dram[:, :, HALF * h : HALF * (h + 1), :].rearrange("g p n t -> p g (n t)")
+            )
+            return t
+
+        w0.append(load_w("w0", w0_words, 0))
+        w0.append(load_w("w0", w0_words, 1))
+        load_x(2)
+        wb.append(load_w("wb", wb_words, 0))
+        wb.append(load_w("wb", wb_words, 1))
+        for i in range(3, CHUNKS):
+            load_x(i)
+
+        s_col = const.tile([P, G, PACK], F32, name="s_col")
+        nc.vector.tensor_copy(out=s_col[:], in_=s_in[:])
+        wr = const.tile([P, G, PACK, R * PACK], U8, name="wr", align_bytes=64)
+        wrs = const.tile([P, PACK, R], U8, name="wrs", align_bytes=64)
+        for q in range(4):
+            nc.vector.tensor_copy(
+                out=wr[:].bitcast(I32)[:, :, :, 32 * q : 32 * q + 32].rearrange("p g t m -> p g m t"),
+                in_=wa[:].bitcast(I32).rearrange("p g (m t) -> p g m t", t=PACK),
+            )
+            nc.vector.tensor_copy(
+                out=wrs[:, :, 32 * q : 32 * q + 32].rearrange("p t m -> p m t"),
+                in_=wasc[:].rearrange("p (m t) -> p m t", t=PACK),
+            )
+        nc.vector.tensor_copy(out=cf[0:E, :], in_=c_in[:])
+        cps = psum.tile([P, 512], F32, tag="misc", name="cps")
+        nc.tensor.transpose(cps[:, 0:P], cf[:], ident[:])
+        ct = const.tile([P, E], F32, name="ct")
+        nc.vector.tensor_scalar(out=ct[:], in0=cps[:, 0:E], scalar1=-0.125, scalar2=None, op0=ALU.mult)
+        csq = const.tile([P, E], F32, name="csq")
+        nc.vector.tensor_tensor(out=csq[:], in0=ct[:], in1=ct[:], op=ALU.mult)
+        cps2 = psum.tile([P, 512], F32, tag="misc", name="cps2")
+        nc.tensor.matmul(cps2[:, 0:E], lhsT=fours[:], rhs=csq[:], start=True, stop=True)
+        nb = const.tile([P, E], F32, name="nb")
+        nc.vector.tensor_copy(out=nb[:], in_=cps2[:, 0:E])
+
+
+        st = {}
+
+        def take(key, shape, dtype, tag, bufs):
+            t = work.tile(shape, dtype, tag=tag, name=tag, bufs=bufs, align_bytes=64)
+            st[key] = t
+            return t
+
+        def widen(i, j):
+            xw = take(("xw", i, j), [P, D], BF16, "xw", 8)
+            nc.vector.tensor_tensor(out=xw[:], in0=x_in[i][:, j, :].bitcast(FP8), in1=xs[:], op=ALU.mult)
+
+        def x_turn(i, j):
+            words = st["xw", i, j][:].bitcast(F32)
+            xt = psum.tile([P, 4, P], F32, tag="sp", name="xt", bufs=SP)
+            st["xt", i, j] = xt
+            for g in range(G):
+                for u in range(2):
+                    nc.tensor.transpose(xt[:, 2 * g + u, :], words[:, 256 * g + u : 256 * (g + 1) : 2], ident[:])
+
+        def x_out(i, j):
+            if ("xb", i) not in st:
+                take(("xb", i), [P, G, NT, 2], F32, "xb", 2)
+            nc.scalar.copy(
+                out=st["xb", i][:, :, P * j : P * (j + 1), :],
+                in_=st["xt", i, j][:].rearrange("p (g u) n -> p g n u", u=2),
+            )
+
+        def x_quant(i):
+            xc = take(("xc", i), [P, G, NT], U32, "xc", 3)
+            xsp = take(("xsp", i), [P, G, NT], U8, "xsp", 3)
+            nc.vector.quantize_mx(
+                out=xc[:].rearrange("p g n -> p (g n)").bitcast(FP8X4),
+                scales=xsp[:].rearrange("p g n -> p (g n)"),
+                in_=st["xb", i][:].rearrange("p g n u -> p (g n u)").bitcast(BF16),
+            )
+
+        def passes(out_ap, lhs, rhs):
+            for g in range(G):
+                lw, ls = lhs(g)
+                rw, rs = rhs(g)
+                nc.tensor.matmul_mx(
+                    out=out_ap, lhsT=lw.bitcast(FP8X4), lhsT_scale=ls, rhs=rw.bitcast(FP8X4), rhs_scale=rs,
+                    start=(g == 0), stop=(g == G - 1),
+                )
+
+        def a_mm(i):
+            m = psum.tile([P, 512], F32, tag="misc", name="misc", bufs=1)
+            st["misc", i] = m
+            passes(
+                m[:, 0:NT],
+                lambda g: (wa[:, g, :], wasc[4 * g :, :]),
+                lambda g: (st["xc", i][:, g, :], st["xsp", i][:, g, :]),
+            )
+
+        def a_out(i):
+            a_sb = take(("a", i), [P, NT], F32, "a_sb", 2)
+            nc.scalar.copy(out=a_sb[:], in_=st["misc", i][:, 0:NT])
+
+        def r_mm(i, k):
+            at = psum.tile([P, 2, NT], F32, tag="sp", name="at", bufs=SP)
+            st["at", i, k] = at
+            for v in range(2):
+                t = 2 * k + v
+                passes(
+                    at[:, v, :],
+                    lambda g: (wr[:, g, t, :], wrs[4 * g :, t, :]),
+                    lambda g: (st["xc", i][:, g, :], st["xsp", i][:, g, :]),
+                )
+
+        def r_out(i, k):
+            if ("pl", i) not in st:
+                take(("pl", i), [P, G, PACK, NT], F32, "pl", 2)
+            for v in range(2):
+                t = 2 * k + v
+                for g in range(G):
+                    nc.scalar.activation(
+                        out=st["pl", i][:, g, t, :], in_=st["at", i, k][:, v, :], func=ACT.Copy,
+                        scale=s_col[:, g, t : t + 1],
+                    )
+
+        def g_dots(i):
+            for j in range(J):
+                nc.tensor.matmul(
+                    st["misc", i][:, NT + E * j : NT + E * (j + 1)], lhsT=st["a", i][:, P * j : P * (j + 1)],
+                    rhs=ct[:], start=True, stop=True,
+                )
+
+        def g_logits(i):
+            l = take(("l", i), [P, J, E], F32, "l", 2)
+            nc.vector.tensor_tensor(
+                out=l[:],
+                in0=st["misc", i][:, NT : NT + J * E].rearrange("p (j e) -> p j e", e=E),
+                in1=nb[:].unsqueeze(1).to_broadcast([P, J, E]),
+                op=ALU.add,
+            )
+
+        def g_min(i):
+            mn = take(("mn", i), [P, J], F32, "mn", 2)
+            nc.vector.tensor_reduce(out=mn[:], in_=st["l", i][:], axis=AX.X, op=ALU.min)
+
+        def g_exp(i):
+            ex = take(("ex", i), [P, J, E], F32, "ex", 2)
+            sm = take(("sm", i), [P, J], F32, "sm", 2)
+            for j in range(J):
+                nc.scalar.activation(
+                    out=ex[:, j, :], in_=st["l", i][:, j, :], func=ACT.Exp, scale=-1.0,
+                    bias=st["mn", i][:, j : j + 1], accum_out=sm[:, j : j + 1],
+                )
+
+        def g_inv(i):
+            ri = take(("ri", i), [P, J], F32, "ri", 2)
+            nc.vector.reciprocal(out=ri[:], in_=st["sm", i][:])
+
+        def g_spread(i):
+            rep = take(("rep", i), [P, J, E, 32], F32, "rep", 2)
+            for j in range(J):
+                nc.scalar.activation(
+                    out=rep[:, j], in_=st["ex", i][:, j, :].unsqueeze(2).to_broadcast([P, E, 32]), func=ACT.Copy,
+                    scale=st["ri", i][:, j : j + 1],
+                )
+
+        def g_turn(i):
+            gp = psum.tile([P, G, NT], F32, tag="gp", name="gp", bufs=1)
+            st["gp", i] = gp
+            for g in range(G):
+                for j in range(J):
+                    nc.tensor.transpose(
+                        gp[:, g, P * j : P * (j + 1)],
+                        st["rep", i][:, j, 4 * g : 4 * g + 4, :].rearrange("p e r -> p (e r)"),
+                        ident[:],
+                    )
+
+        def z_mul(i, g):
+            if ("z", i) not in st:
+                take(("z", i), [P, G, NT, PACK], BF16, "z", 2)
+            nc.vector.tensor_tensor(
+                out=st["z", i][:, g].rearrange("p (c v) t -> p c t v", v=ZV),
+                in0=st["pl", i][:, g].rearrange("p t (c v) -> p c t v", v=ZV),
+                in1=st["gp", i][:, g, :].rearrange("p (c v) -> p c v", v=ZV).unsqueeze(2).to_broadcast(
+                    [P, NT // ZV, PACK, ZV]
+                ),
+                op=ALU.mult,
+            )
+
+        def z_quant(i):
+            zc = take(("zc", i), [P, G, NT], U32, "zc", 2)
+            zsp = take(("zsp", i), [P, G, NT], U8, "zsp", 2)
+            nc.vector.quantize_mx(
+                out=zc[:].rearrange("p g n -> p (g n)").bitcast(FP8X4),
+                scales=zsp[:].rearrange("p g n -> p (g n)"),
+                in_=st["z", i][:].rearrange("p g n t -> p (g n t)"),
+            )
+
+        def base_mm(i, j, h):
+            acc = psum.tile([P, HALF], F32, tag="sp", name="acc", bufs=SP)
+            st["acc", i, j, h] = acc
+            cols = slice(P * j, P * (j + 1))
+            passes(
+                acc[:],
+                lambda g: (st["xc", i][:, g, cols], st["xsp", i][:, g, cols]),
+                lambda g: (w0[h][:, g, :], w0sc[4 * g :, HALF * h : HALF * (h + 1)]),
+            )
+
+        def base_out(i, j, h):
+            t = take(("base", i, j, h), [P, HALF], F32, "base", 12)
+            nc.scalar.copy(out=t[:], in_=st["acc", i, j, h][:])
+
+        def low_mm(i, j, h):
+            acc = psum.tile([P, HALF], F32, tag="ob", name="ob", bufs=OB)
+            st["ob", i, j, h] = acc
+            cols = slice(P * j, P * (j + 1))
+            passes(
+                acc[:],
+                lambda g: (st["zc", i][:, g, cols], st["zsp", i][:, g, cols]),
+                lambda g: (wb[h][:, g, :], wbsc[4 * g :, HALF * h : HALF * (h + 1)]),
+            )
+
+        def low_out(i, j, h):
+            o = take(("o", i, j, h), [P, HALF], F32, "o", 8)
+            nc.vector.scalar_tensor_tensor(
+                out=o[:], in0=st["ob", i, j, h][:], scalar=1.5, in1=st["base", i, j, h][:], op0=ALU.mult, op1=ALU.add
+            )
+            nc.sync.dma_start(
+                out=out[NT * i : NT * (i + 1), :].rearrange("(p j) f -> p j f", j=J)[
+                    :, j, HALF * h : HALF * (h + 1)
+                ],
+                in_=o[:],
+            )
+
+        order = [
+            (low_mm, 3, 0, 1),
+            (x_quant, 1),
+            (widen, -1, 0),
+            (x_turn, 0, 0),
+            (x_turn, 0, 1),
+            (g_turn, 2),
+            (a_mm, 1),
+            (low_mm, 3, 1, 0),
+            (x_out, 0, 0),
+            (base_mm, 1, 0, 0),
+            (r_mm, 1, 0),
+            (base_mm, 1, 1, 1),
+            (x_out, 0, 1),
+            (a_out, 1),
+            (low_out, 3, 0, 1),
+            (g_dots, 1),
+            (base_out, 1, 0, 0),
+            (low_mm, 3, 1, 1),
+            (z_mul, 2, 1),
+            (z_mul, 2, 0),
+            (low_out, 3, 1, 0),
+            (g_logits, 1),
+            (z_quant, 2),
+            (r_out, 1, 0),
+            (g_min, 1),
+            (low_out, 3, 1, 1),
+            (base_mm, 1, 0, 1),
+            (base_mm, 1, 1, 0),
+            (base_out, 1, 1, 1),
+            (low_mm, 3, 0, 0),
+            (widen, -1, 1),
+            (g_exp, 1),
+            (base_out, 1, 0, 1),
+            (g_inv, 1),
+            (g_spread, 1),
+            (r_mm, 1, 1),
+            (r_out, 1, 1),
+            (low_out, 3, 0, 0),
+            (base_out, 1, 1, 0),
+        ]
+        first = min(r[1] for r in order)
+        last = max(r[1] for r in order)
+        with tc.manual_schedule():
+            for step in range(first, CHUNKS + last):
+                for row in order:
+                    i = step - row[1]
+                    if 0 <= i < CHUNKS:
+                        row[0](i, *row[2:])

@@ -24,9 +24,11 @@ CHUNKS = T // NT
 G = 2
 PACK = 4
 HALF = 512
-SP = 4
-OB = 2
-ZV = 4
+SP = 6
+OB = 6
+XCB = 8
+XPERM = False
+GP_ADDS = ((1, 1),)
 
 
 def tile_hydraloraprototyperouted_w8_kernel(
@@ -44,6 +46,8 @@ def tile_hydraloraprototyperouted_w8_kernel(
         wbsc = const.tile([P, F], U8, name="wbsc", align_bytes=64)
         wasc = const.tile([P, R], U8, name="wasc", align_bytes=64)
         cf = const.tile([P, P], F32, name="cf")
+        s_row = const.tile([P, E * R], BF16, name="s_row")
+        nc.gpsimd.memset(s_row[:], 0.0)
         for t in (wasc, w0sc, wbsc):
             nc.gpsimd.memset(t[:].bitcast(I32), 0)
         nc.gpsimd.memset(cf[:], 0.0)
@@ -64,18 +68,16 @@ def tile_hydraloraprototyperouted_w8_kernel(
                     in_=dram[:, 4 * q : 4 * q + 4, :].bitcast(I32),
                 )
 
+        nc.scalar.dma_start(out=xs[:], in_=x_scale.rearrange("o k -> (o k)").partition_broadcast(P))
+        c_in = const.tile([E, R], BF16, name="c_in")
+        nc.scalar.dma_start(out=c_in[:], in_=c)
+        nc.scalar.dma_start(out=s_row[0:1, :], in_=s.rearrange("(o k) -> o k", o=1))
         load_x(0)
-        nc.sync.dma_start(out=xs[:], in_=x_scale.rearrange("o k -> (o k)").partition_broadcast(P))
         load_scales(wasc, wa_scales)
         wa = const.tile([P, G, R * PACK], U8, name="wa", align_bytes=64)
         nc.sync.dma_start(out=wa[:], in_=wa_words.rearrange("g p n t -> p g (n t)"))
-        load_scales(w0sc, w0_scales)
-        load_scales(wbsc, wb_scales)
-        c_in = const.tile([E, R], BF16, name="c_in")
-        nc.sync.dma_start(out=c_in[:], in_=c)
-        s_in = const.tile([P, G, PACK], BF16, name="s_in")
-        nc.sync.dma_start(out=s_in[:], in_=s.rearrange("(g p t) -> p g t", p=P, t=PACK))
         load_x(1)
+        load_scales(w0sc, w0_scales)
         w0 = []
         wb = []
 
@@ -89,35 +91,58 @@ def tile_hydraloraprototyperouted_w8_kernel(
         w0.append(load_w("w0", w0_words, 0))
         w0.append(load_w("w0", w0_words, 1))
         load_x(2)
+        load_scales(wbsc, wb_scales)
         wb.append(load_w("wb", wb_words, 0))
         wb.append(load_w("wb", wb_words, 1))
         for i in range(3, CHUNKS):
             load_x(i)
 
-        s_col = const.tile([P, G, PACK], F32, name="s_col")
-        nc.vector.tensor_copy(out=s_col[:], in_=s_in[:])
-        wr = const.tile([P, G, PACK, R * PACK], U8, name="wr", align_bytes=64)
-        wrs = const.tile([P, PACK, R], U8, name="wrs", align_bytes=64)
-        for q in range(4):
-            nc.vector.tensor_copy(
-                out=wr[:].bitcast(I32)[:, :, :, 32 * q : 32 * q + 32].rearrange("p g t m -> p g m t"),
-                in_=wa[:].bitcast(I32).rearrange("p g (m t) -> p g m t", t=PACK),
-            )
-            nc.vector.tensor_copy(
-                out=wrs[:, :, 32 * q : 32 * q + 32].rearrange("p t m -> p m t"),
-                in_=wasc[:].rearrange("p (m t) -> p m t", t=PACK),
-            )
-        nc.vector.tensor_copy(out=cf[0:E, :], in_=c_in[:])
-        cps = psum.tile([P, 512], F32, tag="misc", name="cps")
-        nc.tensor.transpose(cps[:, 0:P], cf[:], ident[:])
+        ones = const.tile([P, P], BF16, name="ones")
+        nc.gpsimd.memset(ones[:], 1.0)
+        wr = const.tile([P, G, R * PACK], U8, name="wr", align_bytes=64)
+        wrs = const.tile([P, R], U8, name="wrs", align_bytes=64)
+        s_perm = const.tile([P, E, 2, 64], F32, name="s_perm")
         ct = const.tile([P, E], F32, name="ct")
-        nc.vector.tensor_scalar(out=ct[:], in0=cps[:, 0:E], scalar1=-0.125, scalar2=None, op0=ALU.mult)
         csq = const.tile([P, E], F32, name="csq")
-        nc.vector.tensor_tensor(out=csq[:], in0=ct[:], in1=ct[:], op=ALU.mult)
-        cps2 = psum.tile([P, 512], F32, tag="misc", name="cps2")
-        nc.tensor.matmul(cps2[:, 0:E], lhsT=fours[:], rhs=csq[:], start=True, stop=True)
         nb = const.tile([P, E], F32, name="nb")
-        nc.vector.tensor_copy(out=nb[:], in_=cps2[:, 0:E])
+        nc.gpsimd.tensor_copy(out=cf[0:E, :], in_=c_in[:])
+
+        def k_wr(i):
+            for g in range(G):
+                nc.vector.tensor_copy(
+                    out=wr[:, g, :].bitcast(I32).rearrange("p (u m v) -> p m u v", u=2, v=2),
+                    in_=wa[:, g, :].bitcast(I32).rearrange("p (m u v) -> p m u v", u=2, v=2),
+                )
+            nc.vector.tensor_copy(
+                out=wrs[:].rearrange("p (u m v) -> p m u v", u=2, v=2),
+                in_=wasc[:].rearrange("p (m u v) -> p m u v", u=2, v=2),
+            )
+
+        def k_mm(i):
+            st["cps"] = psum.tile([P, 2 * NT], F32, tag="misc", name="cps", bufs=2)
+            nc.tensor.transpose(st["cps"][:, 0:P], cf[:], ident[:])
+            for g in range(G):
+                sps = psum.tile([P, HALF], F32, tag="sp", name="sps", bufs=SP)
+                st["sps", g] = sps
+                nc.tensor.matmul(sps[:], lhsT=ones[:], rhs=s_row[:, HALF * g : HALF * (g + 1)], start=True, stop=True)
+
+        def k_ct(i):
+            nc.scalar.activation(out=ct[:], in_=st["cps"][:, 0:E], func=ACT.Copy, scale=-0.125)
+            nc.gpsimd.tensor_tensor(out=csq[:], in0=ct[:], in1=ct[:], op=ALU.mult)
+
+        def k_out(i):
+            for g in range(G):
+                for u in range(2):
+                    nc.scalar.copy(
+                        out=s_perm[:, 4 * g : 4 * g + 4, u, :].rearrange("p e (m v) -> p e m v", v=2),
+                        in_=st["sps", g][:].rearrange("p (e m u v) -> p e m u v", e=4, u=2, v=2)[:, :, :, u, :],
+                    )
+
+        def k_bias(i):
+            nc.tensor.matmul(st["cps"][:, P : P + E], lhsT=fours[:], rhs=csq[:], start=True, stop=True)
+
+        def k_bias_out(i):
+            nc.scalar.copy(out=nb[:], in_=st["cps"][:, P : P + E])
 
 
         st = {}
@@ -131,30 +156,38 @@ def tile_hydraloraprototyperouted_w8_kernel(
             xw = take(("xw", i, j), [P, D], BF16, "xw", 8)
             nc.vector.tensor_tensor(out=xw[:], in0=x_in[i][:, j, :].bitcast(FP8), in1=xs[:], op=ALU.mult)
 
+        def x_perm(i, j):
+            xp = take(("xp", i, j), [P, G, 2, P], F32, "xp", 4)
+            nc.scalar.copy(
+                out=xp[:], in_=st["xw", i, j][:].bitcast(F32).rearrange("p (g k u) -> p g u k", g=G, u=2)
+            )
+
         def x_turn(i, j):
-            words = st["xw", i, j][:].bitcast(F32)
             xt = psum.tile([P, 4, P], F32, tag="sp", name="xt", bufs=SP)
             st["xt", i, j] = xt
             for g in range(G):
                 for u in range(2):
-                    nc.tensor.transpose(xt[:, 2 * g + u, :], words[:, 256 * g + u : 256 * (g + 1) : 2], ident[:])
+                    if XPERM:
+                        src = st["xp", i, j][:, g, u, :]
+                    else:
+                        src = st["xw", i, j][:].bitcast(F32)[:, 256 * g + u : 256 * (g + 1) : 2]
+                    nc.tensor.transpose(xt[:, 2 * g + u, :], src, ident[:])
 
         def x_out(i, j):
-            if ("xb", i) not in st:
-                take(("xb", i), [P, G, NT, 2], F32, "xb", 2)
-            nc.scalar.copy(
-                out=st["xb", i][:, :, P * j : P * (j + 1), :],
-                in_=st["xt", i, j][:].rearrange("p (g u) n -> p g n u", u=2),
+            xb = take(("xb", i, j), [P, G, P, 2], F32, "xb", 6)
+            nc.scalar.copy(out=xb[:], in_=st["xt", i, j][:].rearrange("p (g u) n -> p g n u", u=2))
+
+        def quant(i, j, src, name, bufs):
+            codes = take((name, i, j), [P, G, P], U32, name, bufs)
+            scales = take((name + "s", i, j), [P, G, P], U8, name + "s", bufs)
+            nc.vector.quantize_mx(
+                out=codes[:].rearrange("p g n -> p (g n)").bitcast(FP8X4),
+                scales=scales[:].rearrange("p g n -> p (g n)"),
+                in_=st[src, i, j][:].rearrange("p g n u -> p (g n u)").bitcast(BF16),
             )
 
-        def x_quant(i):
-            xc = take(("xc", i), [P, G, NT], U32, "xc", 3)
-            xsp = take(("xsp", i), [P, G, NT], U8, "xsp", 3)
-            nc.vector.quantize_mx(
-                out=xc[:].rearrange("p g n -> p (g n)").bitcast(FP8X4),
-                scales=xsp[:].rearrange("p g n -> p (g n)"),
-                in_=st["xb", i][:].rearrange("p g n u -> p (g n u)").bitcast(BF16),
-            )
+        def x_quant(i, j):
+            quant(i, j, "xb", "xc", XCB)
 
         def passes(out_ap, lhs, rhs):
             for g in range(G):
@@ -166,44 +199,31 @@ def tile_hydraloraprototyperouted_w8_kernel(
                 )
 
         def a_mm(i):
-            m = psum.tile([P, 512], F32, tag="misc", name="misc", bufs=1)
+            m = psum.tile([P, 2 * NT], F32, tag="misc", name="misc", bufs=2)
             st["misc", i] = m
-            passes(
-                m[:, 0:NT],
-                lambda g: (wa[:, g, :], wasc[4 * g :, :]),
-                lambda g: (st["xc", i][:, g, :], st["xsp", i][:, g, :]),
-            )
-
-        def a_out(i):
-            a_sb = take(("a", i), [P, NT], F32, "a_sb", 2)
-            nc.scalar.copy(out=a_sb[:], in_=st["misc", i][:, 0:NT])
-
-        def r_mm(i, k):
-            at = psum.tile([P, 2, NT], F32, tag="sp", name="at", bufs=SP)
-            st["at", i, k] = at
-            for v in range(2):
-                t = 2 * k + v
+            for j in range(J):
                 passes(
-                    at[:, v, :],
-                    lambda g: (wr[:, g, t, :], wrs[4 * g :, t, :]),
-                    lambda g: (st["xc", i][:, g, :], st["xsp", i][:, g, :]),
+                    m[:, P * j : P * (j + 1)],
+                    lambda g: (wa[:, g, :], wasc[4 * g :, :]),
+                    lambda g: (st["xc", i, j][:, g, :], st["xcs", i, j][:, g, :]),
                 )
 
-        def r_out(i, k):
-            if ("pl", i) not in st:
-                take(("pl", i), [P, G, PACK, NT], F32, "pl", 2)
-            for v in range(2):
-                t = 2 * k + v
-                for g in range(G):
-                    nc.scalar.activation(
-                        out=st["pl", i][:, g, t, :], in_=st["at", i, k][:, v, :], func=ACT.Copy,
-                        scale=s_col[:, g, t : t + 1],
-                    )
+        def t_mm(i):
+            for j in range(J):
+                passes(
+                    st["misc", i][:, NT + P * j : NT + P * (j + 1)],
+                    lambda g: (st["xc", i, j][:, g, :], st["xcs", i, j][:, g, :]),
+                    lambda g: (wr[:, g, :], wrs[4 * g :, :]),
+                )
+
+        def a_out(i):
+            a_sb = take(("a", i), [P, NT], F32, "a_sb", 3)
+            nc.scalar.copy(out=a_sb[:], in_=st["misc", i][:, 0:NT])
 
         def g_dots(i):
             for j in range(J):
                 nc.tensor.matmul(
-                    st["misc", i][:, NT + E * j : NT + E * (j + 1)], lhsT=st["a", i][:, P * j : P * (j + 1)],
+                    st["misc", i][:, E * j : E * (j + 1)], lhsT=st["a", i][:, P * j : P * (j + 1)],
                     rhs=ct[:], start=True, stop=True,
                 )
 
@@ -211,7 +231,7 @@ def tile_hydraloraprototyperouted_w8_kernel(
             l = take(("l", i), [P, J, E], F32, "l", 2)
             nc.vector.tensor_tensor(
                 out=l[:],
-                in0=st["misc", i][:, NT : NT + J * E].rearrange("p (j e) -> p j e", e=E),
+                in0=st["misc", i][:, 0 : J * E].rearrange("p (j e) -> p j e", e=E),
                 in1=nb[:].unsqueeze(1).to_broadcast([P, J, E]),
                 op=ALU.add,
             )
@@ -233,128 +253,148 @@ def tile_hydraloraprototyperouted_w8_kernel(
             ri = take(("ri", i), [P, J], F32, "ri", 2)
             nc.vector.reciprocal(out=ri[:], in_=st["sm", i][:])
 
-        def g_spread(i):
-            rep = take(("rep", i), [P, J, E, 32], F32, "rep", 2)
+        def g_norm(i):
+            gn = take(("gn", i), [P, J, E], F32, "gn", 2)
             for j in range(J):
                 nc.scalar.activation(
-                    out=rep[:, j], in_=st["ex", i][:, j, :].unsqueeze(2).to_broadcast([P, E, 32]), func=ACT.Copy,
-                    scale=st["ri", i][:, j : j + 1],
+                    out=gn[:, j, :], in_=st["ex", i][:, j, :], func=ACT.Copy, scale=st["ri", i][:, j : j + 1]
                 )
 
-        def g_turn(i):
-            gp = psum.tile([P, G, NT], F32, tag="gp", name="gp", bufs=1)
-            st["gp", i] = gp
-            for g in range(G):
-                for j in range(J):
-                    nc.tensor.transpose(
-                        gp[:, g, P * j : P * (j + 1)],
-                        st["rep", i][:, j, 4 * g : 4 * g + 4, :].rearrange("p e r -> p (e r)"),
-                        ident[:],
-                    )
+        def z_mul(i, j, g):
+            if ("zw", i, j) not in st:
+                take(("zw", i, j), [P, G, 2, 4, 64], BF16, "zw", 6)
+            for q in range(4):
+                e = 4 * g + q
+                nc.vector.scalar_tensor_tensor(
+                    out=st["zw", i, j][:, g, :, q, :],
+                    in0=st["misc", i][:, NT + P * j : NT + P * (j + 1)].rearrange("p (u k) -> p u k", u=2),
+                    scalar=st["gn", i][:, j, e : e + 1],
+                    in1=s_perm[:, e],
+                    op0=ALU.mult,
+                    op1=ALU.mult,
+                )
 
-        def z_mul(i, g):
-            if ("z", i) not in st:
-                take(("z", i), [P, G, NT, PACK], BF16, "z", 2)
-            nc.vector.tensor_tensor(
-                out=st["z", i][:, g].rearrange("p (c v) t -> p c t v", v=ZV),
-                in0=st["pl", i][:, g].rearrange("p t (c v) -> p c t v", v=ZV),
-                in1=st["gp", i][:, g, :].rearrange("p (c v) -> p c v", v=ZV).unsqueeze(2).to_broadcast(
-                    [P, NT // ZV, PACK, ZV]
-                ),
-                op=ALU.mult,
-            )
+        def z_turn(i, j):
+            words = st["zw", i, j][:].rearrange("p g u q k -> p (g u q k)").bitcast(F32)
+            zt = psum.tile([P, 4, P], F32, tag="sp", name="zt", bufs=SP)
+            st["zt", i, j] = zt
+            for b in range(4):
+                nc.tensor.transpose(zt[:, b, :], words[:, P * b : P * (b + 1)], ident[:])
 
-        def z_quant(i):
-            zc = take(("zc", i), [P, G, NT], U32, "zc", 2)
-            zsp = take(("zsp", i), [P, G, NT], U8, "zsp", 2)
-            nc.vector.quantize_mx(
-                out=zc[:].rearrange("p g n -> p (g n)").bitcast(FP8X4),
-                scales=zsp[:].rearrange("p g n -> p (g n)"),
-                in_=st["z", i][:].rearrange("p g n t -> p (g n t)"),
-            )
+        def z_out(i, j):
+            zb = take(("zb", i, j), [P, G, P, 2], F32, "zb", 6)
+            nc.scalar.copy(out=zb[:], in_=st["zt", i, j][:].rearrange("p (g u) n -> p g n u", u=2))
+
+        def z_quant(i, j):
+            quant(i, j, "zb", "zc", 6)
 
         def base_mm(i, j, h):
             acc = psum.tile([P, HALF], F32, tag="sp", name="acc", bufs=SP)
             st["acc", i, j, h] = acc
-            cols = slice(P * j, P * (j + 1))
             passes(
                 acc[:],
-                lambda g: (st["xc", i][:, g, cols], st["xsp", i][:, g, cols]),
+                lambda g: (st["xc", i, j][:, g, :], st["xcs", i, j][:, g, :]),
                 lambda g: (w0[h][:, g, :], w0sc[4 * g :, HALF * h : HALF * (h + 1)]),
             )
 
         def base_out(i, j, h):
-            t = take(("base", i, j, h), [P, HALF], F32, "base", 12)
+            t = take(("base", i, j, h), [P, HALF], F32, "base", 16)
             nc.scalar.copy(out=t[:], in_=st["acc", i, j, h][:])
 
         def low_mm(i, j, h):
-            acc = psum.tile([P, HALF], F32, tag="ob", name="ob", bufs=OB)
+            acc = psum.tile([P, HALF], F32, tag="sp", name="ob", bufs=SP)
             st["ob", i, j, h] = acc
-            cols = slice(P * j, P * (j + 1))
             passes(
                 acc[:],
-                lambda g: (st["zc", i][:, g, cols], st["zsp", i][:, g, cols]),
+                lambda g: (st["zc", i, j][:, g, :], st["zcs", i, j][:, g, :]),
                 lambda g: (wb[h][:, g, :], wbsc[4 * g :, HALF * h : HALF * (h + 1)]),
             )
 
         def low_out(i, j, h):
-            o = take(("o", i, j, h), [P, HALF], F32, "o", 8)
-            nc.vector.scalar_tensor_tensor(
-                out=o[:], in0=st["ob", i, j, h][:], scalar=1.5, in1=st["base", i, j, h][:], op0=ALU.mult, op1=ALU.add
-            )
+            o = take(("o", i, j, h), [P, HALF], F32, "o", 12)
+            if (j, h) in GP_ADDS and i < CHUNKS - 1:
+                lo = take(("lo", i, j, h), [P, HALF], F32, "lo", 6)
+                nc.scalar.activation(out=lo[:], in_=st["ob", i, j, h][:], func=ACT.Copy, scale=1.5)
+            else:
+                nc.vector.scalar_tensor_tensor(
+                    out=o[:], in0=st["ob", i, j, h][:], scalar=1.5, in1=st["base", i, j, h][:], op0=ALU.mult, op1=ALU.add
+                )
+                store(i, j, h)
+
+        def store(i, j, h):
             nc.sync.dma_start(
                 out=out[NT * i : NT * (i + 1), :].rearrange("(p j) f -> p j f", j=J)[
                     :, j, HALF * h : HALF * (h + 1)
                 ],
-                in_=o[:],
+                in_=st["o", i, j, h][:],
             )
 
+        def low_add(i, j, h):
+            if i < CHUNKS - 1:
+                nc.gpsimd.tensor_tensor(
+                    out=st["o", i, j, h][:], in0=st["lo", i, j, h][:], in1=st["base", i, j, h][:], op=ALU.add
+                )
+                store(i, j, h)
+
+
         order = [
-            (low_mm, 3, 0, 1),
-            (x_quant, 1),
-            (widen, -1, 0),
-            (x_turn, 0, 0),
-            (x_turn, 0, 1),
-            (g_turn, 2),
-            (a_mm, 1),
-            (low_mm, 3, 1, 0),
-            (x_out, 0, 0),
+            (k_mm, -1),
+            (widen, 0, 1),
+            (low_add, 5, 1, 1),
+            (z_mul, 2, 1, 0),
             (base_mm, 1, 0, 0),
-            (r_mm, 1, 0),
-            (base_mm, 1, 1, 1),
-            (x_out, 0, 1),
+            (z_mul, 2, 0, 1),
+            (a_mm, 1),
+            (z_mul, 2, 1, 1),
+            (k_ct, 0),
+            (low_mm, 3, 1, 0),
+            (z_mul, 2, 0, 0),
+            (x_turn, 0, 0),
             (a_out, 1),
-            (low_out, 3, 0, 1),
-            (g_dots, 1),
-            (base_out, 1, 0, 0),
-            (low_mm, 3, 1, 1),
-            (z_mul, 2, 1),
-            (z_mul, 2, 0),
+            (x_turn, 0, 1),
+            (k_bias, 0),
             (low_out, 3, 1, 0),
+            (low_mm, 3, 0, 1),
+            (x_out, 0, 0),
+            (g_dots, 1),
+            (widen, -1, 0),
+            (base_out, 1, 0, 0),
+            (x_out, 0, 1),
             (g_logits, 1),
-            (z_quant, 2),
-            (r_out, 1, 0),
+            (z_turn, 2, 1),
+            (k_out, 0),
+            (low_out, 3, 0, 1),
             (g_min, 1),
-            (low_out, 3, 1, 1),
-            (base_mm, 1, 0, 1),
-            (base_mm, 1, 1, 0),
-            (base_out, 1, 1, 1),
+            (z_out, 2, 1),
+            (z_turn, 2, 0),
+            (z_out, 2, 0),
+            (x_quant, 0, 0),
             (low_mm, 3, 0, 0),
-            (widen, -1, 1),
+            (z_quant, 2, 1),
+            (z_quant, 2, 0),
             (g_exp, 1),
-            (base_out, 1, 0, 1),
+            (k_wr, 0),
+            (x_quant, 0, 1),
             (g_inv, 1),
-            (g_spread, 1),
-            (r_mm, 1, 1),
-            (r_out, 1, 1),
             (low_out, 3, 0, 0),
+            (base_mm, 1, 1, 1),
+            (t_mm, 1),
+            (k_bias_out, 0),
+            (low_mm, 3, 1, 1),
+            (g_norm, 1),
+            (base_mm, 1, 0, 1),
+            (base_out, 1, 1, 1),
+            (base_mm, 1, 1, 0),
+            (low_out, 3, 1, 1),
             (base_out, 1, 1, 0),
+            (base_out, 1, 0, 1),
         ]
+        once = (k_wr, k_mm, k_ct, k_out, k_bias, k_bias_out)
         first = min(r[1] for r in order)
         last = max(r[1] for r in order)
         with tc.manual_schedule():
             for step in range(first, CHUNKS + last):
                 for row in order:
                     i = step - row[1]
-                    if 0 <= i < CHUNKS:
+                    if 0 <= i < CHUNKS and (i == 0 or row[0] not in once):
                         row[0](i, *row[2:])

from contextlib import ExitStack

import concourse.mybir as mybir
from concourse.masks import make_identity

T, D, F, R, E = 2048, 1024, 1024, 128, 8
FLOPS = 2 * T * (D * F + D * R + E * R * F)

F32 = mybir.dt.float32
BF16 = mybir.dt.bfloat16
U32 = mybir.dt.uint32
I32 = mybir.dt.int32
U8 = mybir.dt.uint8
FP8 = mybir.dt.float8_e4m3fn
FP8X4 = mybir.dt.float8_e4m3fn_x4
ALU = mybir.AluOpType
ACT = mybir.ActivationFunctionType
AX = mybir.AxisListType

P = 128
J = 2
NT = P * J
CHUNKS = T // NT
G = 2
PACK = 4
HALF = 512
SP = 6
OB = 6
XCB = 8
XPERM = False
GP_ADDS = ((1, 1),)


def tile_hydraloraprototyperouted_w8_kernel(
    tc, x_bytes, x_scale, w0_words, w0_scales, wa_words, wa_scales, c, s, wb_words, wb_scales, out
):
    nc = tc.nc
    with ExitStack() as ctx:
        const = ctx.enter_context(tc.tile_pool(name="const", bufs=1))
        work = ctx.enter_context(tc.tile_pool(name="work", bufs=2))
        psum = ctx.enter_context(tc.psum_pool(name="psum", bufs=1))

        x_in = []
        xs = const.tile([P, D], F32, name="xs", align_bytes=64)
        w0sc = const.tile([P, F], U8, name="w0sc", align_bytes=64)
        wbsc = const.tile([P, F], U8, name="wbsc", align_bytes=64)
        wasc = const.tile([P, R], U8, name="wasc", align_bytes=64)
        cf = const.tile([P, P], F32, name="cf")
        s_row = const.tile([P, E * R], BF16, name="s_row")
        nc.gpsimd.memset(s_row[:], 0.0)
        for t in (wasc, w0sc, wbsc):
            nc.gpsimd.memset(t[:].bitcast(I32), 0)
        nc.gpsimd.memset(cf[:], 0.0)
        ident = const.tile([P, P], F32, name="ident")
        make_identity(nc, ident[:])
        fours = const.tile([P, P], F32, name="fours")
        nc.gpsimd.memset(fours[:], 4.0)

        def load_x(i):
            t = const.tile([P, J, D], U8, name="x_in%d" % i, align_bytes=64)
            nc.sync.dma_start(out=t[:], in_=x_bytes[NT * i : NT * (i + 1), :].rearrange("(p j) k -> p j k", j=J))
            x_in.append(t)

        def load_scales(tile, dram):
            for q in range(4):
                nc.sync.dma_start(
                    out=tile[32 * q : 32 * q + 8, :].bitcast(I32),
                    in_=dram[:, 4 * q : 4 * q + 4, :].bitcast(I32),
                )

        nc.scalar.dma_start(out=xs[:], in_=x_scale.rearrange("o k -> (o k)").partition_broadcast(P))
        c_in = const.tile([E, R], BF16, name="c_in")
        nc.scalar.dma_start(out=c_in[:], in_=c)
        nc.scalar.dma_start(out=s_row[0:1, :], in_=s.rearrange("(o k) -> o k", o=1))
        load_x(0)
        load_scales(wasc, wa_scales)
        wa = const.tile([P, G, R * PACK], U8, name="wa", align_bytes=64)
        nc.sync.dma_start(out=wa[:], in_=wa_words.rearrange("g p n t -> p g (n t)"))
        load_x(1)
        load_scales(w0sc, w0_scales)
        w0 = []
        wb = []

        def load_w(name, dram, h):
            t = const.tile([P, G, HALF * PACK], U8, name="%s%d" % (name, h), align_bytes=64)
            nc.sync.dma_start(
                out=t[:], in_=dram[:, :, HALF * h : HALF * (h + 1), :].rearrange("g p n t -> p g (n t)")
            )
            return t

        w0.append(load_w("w0", w0_words, 0))
        w0.append(load_w("w0", w0_words, 1))
        load_x(2)
        load_scales(wbsc, wb_scales)
        wb.append(load_w("wb", wb_words, 0))
        wb.append(load_w("wb", wb_words, 1))
        for i in range(3, CHUNKS):
            load_x(i)

        ones = const.tile([P, P], BF16, name="ones")
        nc.gpsimd.memset(ones[:], 1.0)
        wr = const.tile([P, G, R * PACK], U8, name="wr", align_bytes=64)
        wrs = const.tile([P, R], U8, name="wrs", align_bytes=64)
        s_perm = const.tile([P, E, 2, 64], F32, name="s_perm")
        ct = const.tile([P, E], F32, name="ct")
        csq = const.tile([P, E], F32, name="csq")
        nb = const.tile([P, E], F32, name="nb")
        nc.gpsimd.tensor_copy(out=cf[0:E, :], in_=c_in[:])

        def k_wr(i):
            for g in range(G):
                nc.vector.tensor_copy(
                    out=wr[:, g, :].bitcast(I32).rearrange("p (u m v) -> p m u v", u=2, v=2),
                    in_=wa[:, g, :].bitcast(I32).rearrange("p (m u v) -> p m u v", u=2, v=2),
                )
            nc.vector.tensor_copy(
                out=wrs[:].rearrange("p (u m v) -> p m u v", u=2, v=2),
                in_=wasc[:].rearrange("p (m u v) -> p m u v", u=2, v=2),
            )

        def k_mm(i):
            st["cps"] = psum.tile([P, 2 * NT], F32, tag="misc", name="cps", bufs=2)
            nc.tensor.transpose(st["cps"][:, 0:P], cf[:], ident[:])
            for g in range(G):
                sps = psum.tile([P, HALF], F32, tag="sp", name="sps", bufs=SP)
                st["sps", g] = sps
                nc.tensor.matmul(sps[:], lhsT=ones[:], rhs=s_row[:, HALF * g : HALF * (g + 1)], start=True, stop=True)

        def k_ct(i):
            nc.scalar.activation(out=ct[:], in_=st["cps"][:, 0:E], func=ACT.Copy, scale=-0.125)
            nc.gpsimd.tensor_tensor(out=csq[:], in0=ct[:], in1=ct[:], op=ALU.mult)

        def k_out(i):
            for g in range(G):
                for u in range(2):
                    nc.scalar.copy(
                        out=s_perm[:, 4 * g : 4 * g + 4, u, :].rearrange("p e (m v) -> p e m v", v=2),
                        in_=st["sps", g][:].rearrange("p (e m u v) -> p e m u v", e=4, u=2, v=2)[:, :, :, u, :],
                    )

        def k_bias(i):
            nc.tensor.matmul(st["cps"][:, P : P + E], lhsT=fours[:], rhs=csq[:], start=True, stop=True)

        def k_bias_out(i):
            nc.scalar.copy(out=nb[:], in_=st["cps"][:, P : P + E])


        st = {}

        def take(key, shape, dtype, tag, bufs):
            t = work.tile(shape, dtype, tag=tag, name=tag, bufs=bufs, align_bytes=64)
            st[key] = t
            return t

        def widen(i, j):
            xw = take(("xw", i, j), [P, D], BF16, "xw", 8)
            nc.vector.tensor_tensor(out=xw[:], in0=x_in[i][:, j, :].bitcast(FP8), in1=xs[:], op=ALU.mult)

        def x_perm(i, j):
            xp = take(("xp", i, j), [P, G, 2, P], F32, "xp", 4)
            nc.scalar.copy(
                out=xp[:], in_=st["xw", i, j][:].bitcast(F32).rearrange("p (g k u) -> p g u k", g=G, u=2)
            )

        def x_turn(i, j):
            xt = psum.tile([P, 4, P], F32, tag="sp", name="xt", bufs=SP)
            st["xt", i, j] = xt
            for g in range(G):
                for u in range(2):
                    if XPERM:
                        src = st["xp", i, j][:, g, u, :]
                    else:
                        src = st["xw", i, j][:].bitcast(F32)[:, 256 * g + u : 256 * (g + 1) : 2]
                    nc.tensor.transpose(xt[:, 2 * g + u, :], src, ident[:])

        def x_out(i, j):
            xb = take(("xb", i, j), [P, G, P, 2], F32, "xb", 6)
            nc.scalar.copy(out=xb[:], in_=st["xt", i, j][:].rearrange("p (g u) n -> p g n u", u=2))

        def quant(i, j, src, name, bufs):
            codes = take((name, i, j), [P, G, P], U32, name, bufs)
            scales = take((name + "s", i, j), [P, G, P], U8, name + "s", bufs)
            nc.vector.quantize_mx(
                out=codes[:].rearrange("p g n -> p (g n)").bitcast(FP8X4),
                scales=scales[:].rearrange("p g n -> p (g n)"),
                in_=st[src, i, j][:].rearrange("p g n u -> p (g n u)").bitcast(BF16),
            )

        def x_quant(i, j):
            quant(i, j, "xb", "xc", XCB)

        def passes(out_ap, lhs, rhs):
            for g in range(G):
                lw, ls = lhs(g)
                rw, rs = rhs(g)
                nc.tensor.matmul_mx(
                    out=out_ap, lhsT=lw.bitcast(FP8X4), lhsT_scale=ls, rhs=rw.bitcast(FP8X4), rhs_scale=rs,
                    start=(g == 0), stop=(g == G - 1),
                )

        def a_mm(i):
            m = psum.tile([P, 2 * NT], F32, tag="misc", name="misc", bufs=2)
            st["misc", i] = m
            for j in range(J):
                passes(
                    m[:, P * j : P * (j + 1)],
                    lambda g: (wa[:, g, :], wasc[4 * g :, :]),
                    lambda g: (st["xc", i, j][:, g, :], st["xcs", i, j][:, g, :]),
                )

        def t_mm(i):
            for j in range(J):
                passes(
                    st["misc", i][:, NT + P * j : NT + P * (j + 1)],
                    lambda g: (st["xc", i, j][:, g, :], st["xcs", i, j][:, g, :]),
                    lambda g: (wr[:, g, :], wrs[4 * g :, :]),
                )

        def a_out(i):
            a_sb = take(("a", i), [P, NT], F32, "a_sb", 3)
            nc.scalar.copy(out=a_sb[:], in_=st["misc", i][:, 0:NT])

        def g_dots(i):
            for j in range(J):
                nc.tensor.matmul(
                    st["misc", i][:, E * j : E * (j + 1)], lhsT=st["a", i][:, P * j : P * (j + 1)],
                    rhs=ct[:], start=True, stop=True,
                )

        def g_logits(i):
            l = take(("l", i), [P, J, E], F32, "l", 2)
            nc.vector.tensor_tensor(
                out=l[:],
                in0=st["misc", i][:, 0 : J * E].rearrange("p (j e) -> p j e", e=E),
                in1=nb[:].unsqueeze(1).to_broadcast([P, J, E]),
                op=ALU.add,
            )

        def g_min(i):
            mn = take(("mn", i), [P, J], F32, "mn", 2)
            nc.vector.tensor_reduce(out=mn[:], in_=st["l", i][:], axis=AX.X, op=ALU.min)

        def g_exp(i):
            ex = take(("ex", i), [P, J, E], F32, "ex", 2)
            sm = take(("sm", i), [P, J], F32, "sm", 2)
            for j in range(J):
                nc.scalar.activation(
                    out=ex[:, j, :], in_=st["l", i][:, j, :], func=ACT.Exp, scale=-1.0,
                    bias=st["mn", i][:, j : j + 1], accum_out=sm[:, j : j + 1],
                )

        def g_inv(i):
            ri = take(("ri", i), [P, J], F32, "ri", 2)
            nc.vector.reciprocal(out=ri[:], in_=st["sm", i][:])

        def g_norm(i):
            gn = take(("gn", i), [P, J, E], F32, "gn", 2)
            for j in range(J):
                nc.scalar.activation(
                    out=gn[:, j, :], in_=st["ex", i][:, j, :], func=ACT.Copy, scale=st["ri", i][:, j : j + 1]
                )

        def z_mul(i, j, g):
            if ("zw", i, j) not in st:
                take(("zw", i, j), [P, G, 2, 4, 64], BF16, "zw", 6)
            for q in range(4):
                e = 4 * g + q
                nc.vector.scalar_tensor_tensor(
                    out=st["zw", i, j][:, g, :, q, :],
                    in0=st["misc", i][:, NT + P * j : NT + P * (j + 1)].rearrange("p (u k) -> p u k", u=2),
                    scalar=st["gn", i][:, j, e : e + 1],
                    in1=s_perm[:, e],
                    op0=ALU.mult,
                    op1=ALU.mult,
                )

        def z_turn(i, j):
            words = st["zw", i, j][:].rearrange("p g u q k -> p (g u q k)").bitcast(F32)
            zt = psum.tile([P, 4, P], F32, tag="sp", name="zt", bufs=SP)
            st["zt", i, j] = zt
            for b in range(4):
                nc.tensor.transpose(zt[:, b, :], words[:, P * b : P * (b + 1)], ident[:])

        def z_out(i, j):
            zb = take(("zb", i, j), [P, G, P, 2], F32, "zb", 6)
            nc.scalar.copy(out=zb[:], in_=st["zt", i, j][:].rearrange("p (g u) n -> p g n u", u=2))

        def z_quant(i, j):
            quant(i, j, "zb", "zc", 6)

        def base_mm(i, j, h):
            acc = psum.tile([P, HALF], F32, tag="sp", name="acc", bufs=SP)
            st["acc", i, j, h] = acc
            passes(
                acc[:],
                lambda g: (st["xc", i, j][:, g, :], st["xcs", i, j][:, g, :]),
                lambda g: (w0[h][:, g, :], w0sc[4 * g :, HALF * h : HALF * (h + 1)]),
            )

        def base_out(i, j, h):
            t = take(("base", i, j, h), [P, HALF], F32, "base", 16)
            nc.scalar.copy(out=t[:], in_=st["acc", i, j, h][:])

        def low_mm(i, j, h):
            acc = psum.tile([P, HALF], F32, tag="sp", name="ob", bufs=SP)
            st["ob", i, j, h] = acc
            passes(
                acc[:],
                lambda g: (st["zc", i, j][:, g, :], st["zcs", i, j][:, g, :]),
                lambda g: (wb[h][:, g, :], wbsc[4 * g :, HALF * h : HALF * (h + 1)]),
            )

        def low_out(i, j, h):
            o = take(("o", i, j, h), [P, HALF], F32, "o", 12)
            if (j, h) in GP_ADDS and i < CHUNKS - 1:
                lo = take(("lo", i, j, h), [P, HALF], F32, "lo", 6)
                nc.scalar.activation(out=lo[:], in_=st["ob", i, j, h][:], func=ACT.Copy, scale=1.5)
            else:
                nc.vector.scalar_tensor_tensor(
                    out=o[:], in0=st["ob", i, j, h][:], scalar=1.5, in1=st["base", i, j, h][:], op0=ALU.mult, op1=ALU.add
                )
                store(i, j, h)

        def store(i, j, h):
            nc.sync.dma_start(
                out=out[NT * i : NT * (i + 1), :].rearrange("(p j) f -> p j f", j=J)[
                    :, j, HALF * h : HALF * (h + 1)
                ],
                in_=st["o", i, j, h][:],
            )

        def low_add(i, j, h):
            if i < CHUNKS - 1:
                nc.gpsimd.tensor_tensor(
                    out=st["o", i, j, h][:], in0=st["lo", i, j, h][:], in1=st["base", i, j, h][:], op=ALU.add
                )
                store(i, j, h)


        order = [
            (k_mm, -1),
            (widen, 0, 1),
            (low_add, 5, 1, 1),
            (z_mul, 2, 1, 0),
            (base_mm, 1, 0, 0),
            (z_mul, 2, 0, 1),
            (a_mm, 1),
            (z_mul, 2, 1, 1),
            (k_ct, 0),
            (low_mm, 3, 1, 0),
            (z_mul, 2, 0, 0),
            (x_turn, 0, 0),
            (a_out, 1),
            (x_turn, 0, 1),
            (k_bias, 0),
            (low_out, 3, 1, 0),
            (low_mm, 3, 0, 1),
            (x_out, 0, 0),
            (g_dots, 1),
            (widen, -1, 0),
            (base_out, 1, 0, 0),
            (x_out, 0, 1),
            (g_logits, 1),
            (z_turn, 2, 1),
            (k_out, 0),
            (low_out, 3, 0, 1),
            (g_min, 1),
            (z_out, 2, 1),
            (z_turn, 2, 0),
            (z_out, 2, 0),
            (x_quant, 0, 0),
            (low_mm, 3, 0, 0),
            (z_quant, 2, 1),
            (z_quant, 2, 0),
            (g_exp, 1),
            (k_wr, 0),
            (x_quant, 0, 1),
            (g_inv, 1),
            (low_out, 3, 0, 0),
            (base_mm, 1, 1, 1),
            (t_mm, 1),
            (k_bias_out, 0),
            (low_mm, 3, 1, 1),
            (g_norm, 1),
            (base_mm, 1, 0, 1),
            (base_out, 1, 1, 1),
            (base_mm, 1, 1, 0),
            (low_out, 3, 1, 1),
            (base_out, 1, 1, 0),
            (base_out, 1, 0, 1),
        ]
        once = (k_wr, k_mm, k_ct, k_out, k_bias, k_bias_out)
        first = min(r[1] for r in order)
        last = max(r[1] for r in order)
        with tc.manual_schedule():
            for step in range(first, CHUNKS + last):
                for row in order:
                    i = step - row[1]
                    if 0 <= i < CHUNKS and (i == 0 or row[0] not in once):
                        row[0](i, *row[2:])
